import numpy as np
import ml_dtypes


def mxq(x, axis, fmt="e4m3"):
    dtype, down = {"e4m3": (ml_dtypes.float8_e4m3fn, 7), "e5m2": (ml_dtypes.float8_e5m2, 14)}[fmt]
    v = np.moveaxis(np.asarray(x, np.float32).astype(ml_dtypes.bfloat16).astype(np.float64), axis, -1)
    blocks = v.reshape(v.shape[:-1] + (-1, 32))
    amax = np.abs(blocks).max(-1, keepdims=True)
    byte = np.maximum(np.where(amax > 0, np.frexp(amax)[1] - 1 + 127, 0) - down, 1)
    scale = np.exp2(byte - 127.0)
    codes = (blocks / scale).astype(np.float32).astype(dtype).astype(np.float64)
    return np.moveaxis((codes * scale).reshape(v.shape), -1, axis)


WIDE = False


def mx_kscale(k, group=512):
    if not WIDE:
        return np.ones(k)
    levels = np.array([10, -10, 5, -5, 0])
    if group != 512:
        return np.exp2(np.random.permutation(np.resize(levels, k // group))).repeat(group)
    if k % 512:
        return np.exp2(np.random.permutation(np.resize(levels, k // 32))).repeat(32)
    a = np.empty((k // 512, 16))
    for p in range(k // 512):
        a[p, :8] = np.random.permutation(np.resize(levels, 8))
        for g in range(8):
            far = levels[np.abs(levels - a[p, g]) >= 10]
            a[p, g + 8] = far[np.random.randint(len(far))]
    return np.exp2(a.ravel()).repeat(32)


def f64(x):
    return np.asarray(x).astype(np.float64)


def bf(x):
    return np.asarray(x, np.float32).astype(ml_dtypes.bfloat16)


def planes(Y):
    r, m = Y.shape
    b = f64(bf(Y)).reshape(r // 32, 32, m)
    amax = np.abs(b).max(1)
    byte = np.clip(np.where(amax > 0, np.frexp(amax)[1] - 1 + 127 - 7, 1), 1, 254)
    codes = (b * np.exp2(127.0 - byte)[:, None, :]).reshape(r, m).astype(np.float32).astype(ml_dtypes.float8_e4m3fn).view(np.uint8)
    words = codes.reshape(r // 512, 128, 4, m).transpose(0, 1, 3, 2)
    return np.ascontiguousarray(words), np.ascontiguousarray(byte.astype(np.uint8).reshape(r // 512, 16, m))


G, D, M, N = 2, 256, 256, 512


def setup_inputs():
    n = np.random.standard_normal
    s_d = mx_kscale(D, 0)
    return {
        "x": (n((G, D, N)) * s_d[:, None]).astype(np.float32),
        "w1": (n((G, D, M)) / np.sqrt(D) / s_d[:, None]).astype(np.float32),
        "w2": (n((G, D, M)) / np.sqrt(D) / s_d[:, None]).astype(np.float32),
        "gn": (np.random.uniform(0.5, 2.0, (G, M, 1))).astype(np.float32),
        "dx": (n((G, D, N)) * s_d[:, None]).astype(np.float32),
        "og": (np.random.uniform(0.5, 2.0, (G, M, 1))).astype(np.float32),
        "base": (0.3 * n((G, M, N))).astype(np.float32),
    }


def reference(x, w1, w2, gn, dx, og, base):
    w1q = mxq(f64(w1), 1, "e4m3")
    xq = mxq(f64(x), 1, "e4m3")
    z1 = w1q.transpose(0, 2, 1) @ xq
    dxq = mxq(f64(dx), 1, "e4m3")
    tz1 = w1q.transpose(0, 2, 1) @ dxq
    w2q = mxq(f64(w2), 1, "e4m3")
    z2 = w2q.transpose(0, 2, 1) @ xq
    tz2 = w2q.transpose(0, 2, 1) @ dxq
    mu = np.mean(z1, axis=-1, keepdims=True)
    ce = z1 - mu
    sd = np.sqrt(np.mean(np.square(ce), axis=-1, keepdims=True) + 0.05)
    xmu = np.mean(tz1, axis=-1, keepdims=True)
    xce = tz1 - xmu
    xsd = np.mean(xce * ce * 2.0, axis=-1, keepdims=True) * 0.5 / sd
    xh = (xce - xsd * ce / sd) / sd * f64(gn) * (1.0 - np.square(np.tanh(ce / sd * f64(gn)))) * z2 + tz2 * np.tanh(ce / sd * f64(gn))
    y = xh * f64(og) + f64(base)
    Y = y.reshape(G * M, N)
    words, scales = planes(Y)
    return Y, words, scales

@@ -1,0 +1,300 @@
+from contextlib import ExitStack
+
+import concourse.mybir as mybir
+
+G, D, M, N = 2, 256, 256, 512
+FLOPS = 4 * 2 * G * D * M * N
+
+F32 = mybir.dt.float32
+BF16 = mybir.dt.bfloat16
+I32 = mybir.dt.int32
+U32 = mybir.dt.uint32
+U8 = mybir.dt.uint8
+FP8X4 = mybir.dt.float8_e4m3fn_x4
+ALU = mybir.AluOpType
+ACT = mybir.ActivationFunctionType
+
+P = 128
+ROWS = 64
+PACK = 4
+HALF = N // 2
+EPS = 0.05
+X_SPLIT = 352
+DX_SPLIT = 384
+Y_SPLIT = 176
+
+
+def tile_rows_pl_tnrowcentre_kernel(tc, x, w1, w2, gn, dx, og, base, out_0, out_1, out_2):
+    nc = tc.nc
+    with ExitStack() as ctx:
+        sb = ctx.enter_context(tc.tile_pool(name="sb", bufs=1))
+        ps = ctx.enter_context(tc.psum_pool(name="ps", bufs=1))
+        ctx.enter_context(tc.manual_schedule())
+
+        def new(name, shape, dtype=F32):
+            return sb.tile(shape, dtype, name=name, align_bytes=64)
+
+        def col(name):
+            return [new("%s%d" % (name, i), [P, 1]) for i in range(4)]
+
+        def full(name):
+            return [new("%s%d" % (name, i), [P, N]) for i in range(4)]
+
+        banks = [[ps.tile([P, N], F32, name="bank%d%d" % (g, b)) for b in range(4)] for g in range(G)]
+
+        def load_rows(name, src):
+            width = src.shape[2]
+            raw = new(name, [P, PACK, width])
+            nc.sync.dma_start(out=raw[:], in_=src.rearrange("g (p j) c -> (g p) j c", j=PACK))
+            return raw
+
+        gn_t = new("gn_t", [P, G, 2])
+        og_t = new("og_t", [P, G, 2])
+        x_raw = load_rows("x_raw", x)
+        nc.scalar.dma_start(out=gn_t[:], in_=gn.rearrange("g (q h) o -> q g (h o)", h=2))
+        nc.scalar.dma_start(out=og_t[:], in_=og.rearrange("g (q h) o -> q g (h o)", h=2))
+        w1_raw = load_rows("w1_raw", w1)
+        dx_raw = load_rows("dx_raw", dx)
+        w2_raw = load_rows("w2_raw", w2)
+        base_t = []
+        for g in range(G):
+            t = new("base%d" % g, [P, 2, N])
+            nc.sync.dma_start(out=t[:], in_=base[g].rearrange("(q h) n -> q h n", h=2))
+            base_t.append(t)
+
+        pre = new("pre", [P, 4, 8])
+        mean_fac = new("mean_fac", [P, 4, 2])
+        minus_half = new("minus_half", [P, 1])
+        nc.gpsimd.memset(minus_half[:], -0.5)
+        nc.gpsimd.memset(pre[:, :, 2], -float(N))
+        nc.gpsimd.memset(mean_fac[:, :, 1], -1.0 / N)
+        gn_f = gn_t[:].rearrange("p g h -> p (g h)")
+        og_f = og_t[:].rearrange("p g h -> p (g h)")
+        nc.gpsimd.tensor_scalar(out=mean_fac[:, :, 0], in0=gn_f, scalar1=1.0, scalar2=0.0, op0=ALU.mult, op1=ALU.add)
+        nc.gpsimd.tensor_scalar(out=pre[:, :, 0], in0=gn_f, scalar1=-float(N), scalar2=0.0, op0=ALU.mult, op1=ALU.add)
+        gain = new("gain", [P, 4])
+        nc.gpsimd.tensor_tensor(out=gain[:], in0=gn_f, in1=og_f, op=ALU.mult)
+        nc.gpsimd.tensor_scalar(out=pre[:, :, 1], in0=gain[:], scalar1=-1.0, scalar2=0.0, op0=ALU.mult, op1=ALU.add)
+
+        def v_copy(out, in_):
+            nc.vector.tensor_copy(out=out, in_=in_)
+
+        def s_copy(out, in_):
+            nc.scalar.activation(out=out, in_=in_, func=ACT.Copy)
+
+        def interleave(copy, dst, src, c0, c1):
+            copy(dst[:, c0:c1, :].rearrange("p (c i) j -> p c j i", i=4),
+                 src[:, :, c0:c1].rearrange("p j (c i) -> p c j i", i=4))
+
+        def deal(copy, dst, src, h):
+            copy(dst[:, h].rearrange("p (c i) j -> p c j i", i=2),
+                 src[:].rearrange("p j (c i h) -> p h c j i", i=2, h=2)[:, h])
+
+        def quantise(name, flat):
+            width = flat.shape[1] // PACK
+            codes = new(name + "_codes", [P, width], U32)
+            scales = new(name + "_scales", [P, width], U8)
+            nc.vector.quantize_mx(out=codes[:].bitcast(FP8X4), scales=scales[:], in_=flat)
+            return codes, scales
+
+        def product(i, bank, wq, xq):
+            g, h = divmod(i, 2)
+            rows = slice(ROWS * g, ROWS * (g + 1))
+            cols = slice(P * h, P * (h + 1))
+            nc.tensor.matmul_mx(out=banks[g][bank][:], lhsT=wq[0][rows, cols].bitcast(FP8X4), lhsT_scale=wq[1][rows, cols],
+                                rhs=xq[0][rows, :].bitcast(FP8X4), rhs_scale=xq[1][rows, :], start=True, stop=True)
+
+        x_b = new("x_b", [P, N, PACK], BF16)
+        dx_b = new("dx_b", [P, N, PACK], BF16)
+        w1_b = new("w1_b", [P, 2, P, PACK], BF16)
+        w2_b = new("w2_b", [P, 2, P, PACK], BF16)
+
+        zs, th, sq, q, f, m, e, fb, y = [full(n) for n in ("zs", "th", "sq", "q", "f", "m", "e", "fb", "y")]
+        junk_s, junk_v = full("junk_s"), full("junk_v")
+        nmu, ssq, var, rs, r2, cov, kk, qsum, nqm = [
+            col(n) for n in ("nmu", "ssq", "var", "rs", "r2", "cov", "kk", "qsum", "nqm")]
+        fac = [new("fac%d" % i, [P, 4]) for i in range(4)]
+        z = [new("z%d" % g, [P, PACK, HALF]) for g in range(G)]
+        y_b = [new("y_b%d" % g, [P, HALF, PACK], BF16) for g in range(G)]
+
+        def bank_of(i, what):
+            g, h = divmod(i, 2)
+            return banks[g][{"z1": h, "tz1": 2 + h, "tz2": 2 * h, "z2": 1 - h}[what]]
+
+        def a_copy(i):
+            nc.scalar.activation(out=zs[i][:], in_=bank_of(i, "z1")[:], func=ACT.Copy, scale=-1.0 / N, accum_out=nmu[i][:])
+
+        def a_var(i):
+            nc.scalar.activation(out=junk_s[i][:], in_=zs[i][:], func=ACT.Square, scale=-float(N), bias=nmu[i][:], accum_out=ssq[i][:])
+            nc.scalar.activation(out=pre[:, i, 3:5], in_=mean_fac[:, i, :], func=ACT.Copy, scale=nmu[i][:])
+            nc.scalar.activation(out=var[i][:], in_=ssq[i][:], func=ACT.Copy, scale=1.0 / N, bias=EPS)
+
+        def p_pow(i):
+            nc.gpsimd.tensor_tensor(out=rs[i][:], in0=var[i][:], in1=minus_half[:], op=ALU.pow)
+
+        def a_fac(i):
+            nc.scalar.activation(out=fac[i][:], in_=pre[:, i, 0:4], func=ACT.Copy, scale=rs[i][:])
+            nc.scalar.activation(out=r2[i][:], in_=fac[i][:, 2:3], func=ACT.Copy, scale=rs[i][:])
+
+        def a_tanh(i):
+            nc.scalar.activation(out=th[i][:], in_=zs[i][:], func=ACT.Tanh, scale=fac[i][:, 0:1], bias=fac[i][:, 3:4])
+
+        def a_sq(i):
+            nc.scalar.activation(out=sq[i][:], in_=th[i][:], func=ACT.Square)
+
+        def a_kk(i):
+            nc.scalar.activation(out=kk[i][:], in_=cov[i][:], func=ACT.Copy, scale=r2[i][:])
+
+        def a_nqm(i):
+            nc.scalar.activation(out=nqm[i][:], in_=qsum[i][:], func=ACT.Copy, scale=-1.0 / N)
+
+        def stt(out, in0, scalar, in1, op0, op1, accum_out=None):
+            nc.vector.scalar_tensor_tensor(out=out, in0=in0, scalar=scalar, in1=in1, op0=op0, op1=op1, accum_out=accum_out)
+
+        def v_cov(i):
+            stt(junk_v[i][:], zs[i][:], pre[:, i, 4:5], bank_of(i, "tz1")[:], ALU.add, ALU.mult, cov[i][:])
+
+        def v_q(i):
+            stt(q[i][:], zs[i][:], kk[i][:], bank_of(i, "tz1")[:], ALU.mult, ALU.add, qsum[i][:])
+
+        def v_f(i):
+            g, h = divmod(i, 2)
+            stt(f[i][:], bank_of(i, "tz2")[:], og_t[:, g, h:h + 1], th[i][:], ALU.mult, ALU.mult)
+
+        def v_m(i):
+            stt(m[i][:], sq[i][:], -1.0, bank_of(i, "z2")[:], ALU.add, ALU.mult)
+
+        def v_e(i):
+            stt(e[i][:], q[i][:], nqm[i][:], m[i][:], ALU.add, ALU.mult)
+
+        def add_base(i, eng):
+            g, h = divmod(i, 2)
+            eng.tensor_tensor(out=fb[i][:], in0=f[i][:], in1=base_t[g][:, h, :], op=ALU.add)
+
+        def make_y(i):
+            stt(y[i][:], e[i][:], fac[i][:, 1:2], fb[i][:], ALU.mult, ALU.add)
+
+        def send(i, queues):
+            g, h = divmod(i, 2)
+            k = 0
+            for a in range(2):
+                for b in range(2):
+                    queues[k % len(queues)].dma_start(out=z[g][ROWS * b:ROWS * (b + 1), 2 * a + h, :],
+                                                      in_=y[i][a:P:2, HALF * b:HALF * (b + 1)])
+                    k = k + 1
+            nc.sync.dma_start(out=out_0[M * g:M * (g + 1), :].rearrange("(q h) n -> q h n", h=2)[:, h, :], in_=y[i][:])
+
+        def store_planes(g, yq, queues):
+            codes, scales = yq
+            words = out_1.rearrange("s p n u -> (s p) (n u)").bitcast(I32)
+            bytes4 = out_2.rearrange("s f n -> (s f) n").bitcast(I32)
+            for b in range(2):
+                queues[b % len(queues)].dma_start(out=words[ROWS * g:ROWS * (g + 1), HALF * b:HALF * (b + 1)],
+                                                  in_=codes[ROWS * b:ROWS * (b + 1), :].bitcast(I32))
+            for quad in range(4):
+                b, lo = divmod(quad, 2)
+                f0 = 8 * g + 4 * lo
+                queues[quad % len(queues)].dma_start(out=bytes4[f0:f0 + 4, (HALF // 4) * b:(HALF // 4) * (b + 1)],
+                                                     in_=scales[32 * quad:32 * quad + 4, :].bitcast(I32))
+
+        def flat3(t):
+            return t[:].rearrange("p c j -> p (c j)")
+
+        def flat4(t):
+            return t[:].rearrange("p h c j -> p (h c j)")
+
+        interleave(v_copy, x_b, x_raw, 0, X_SPLIT)
+        interleave(s_copy, x_b, x_raw, X_SPLIT, N)
+        xq = quantise("xq", flat3(x_b))
+        deal(s_copy, w1_b, w1_raw, 0)
+        deal(v_copy, w1_b, w1_raw, 1)
+        w1q = quantise("w1q", flat4(w1_b))
+        for i in (0, 2, 1, 3):
+            product(i, i % 2, w1q, xq)
+        a_copy(0)
+        interleave(v_copy, dx_b, dx_raw, 0, DX_SPLIT)
+        interleave(s_copy, dx_b, dx_raw, DX_SPLIT, N)
+        dxq = quantise("dxq", flat3(dx_b))
+        for i in (0, 2, 1, 3):
+            product(i, 2 + i % 2, w1q, dxq)
+        a_var(0)
+        p_pow(0)
+        a_copy(1)
+        a_var(1)
+        p_pow(1)
+        deal(v_copy, w2_b, w2_raw, 0)
+        deal(v_copy, w2_b, w2_raw, 1)
+        v_cov(0)
+        w2q = quantise("w2q", flat4(w2_b))
+        product(0, 0, w2q, dxq)
+        product(0, 1, w2q, xq)
+        a_fac(0)
+        a_kk(0)
+        a_tanh(0)
+        v_cov(1)
+        v_q(0)
+        product(1, 2, w2q, dxq)
+        a_fac(1)
+        a_kk(1)
+        a_sq(0)
+        a_nqm(0)
+        v_f(0)
+        add_base(0, nc.gpsimd)
+        a_copy(2)
+        a_var(2)
+        p_pow(2)
+        product(1, 0, w2q, xq)
+        product(2, 0, w2q, dxq)
+        v_m(0)
+        v_q(1)
+        v_e(0)
+        v_cov(2)
+        make_y(0)
+        send(0, [nc.sync])
+        a_nqm(1)
+        a_tanh(1)
+        a_sq(1)
+        a_fac(2)
+        a_kk(2)
+        v_f(1)
+        add_base(1, nc.gpsimd)
+        a_copy(3)
+        a_var(3)
+        p_pow(3)
+        product(2, 1, w2q, xq)
+        v_m(1)
+        v_q(2)
+        product(3, 2, w2q, dxq)
+        v_e(1)
+        v_cov(3)
+        make_y(1)
+        send(1, [nc.sync])
+        a_tanh(2)
+        a_nqm(2)
+        a_sq(2)
+        a_fac(3)
+        a_kk(3)
+        a_tanh(3)
+        a_sq(3)
+        v_f(2)
+        add_base(2, nc.gpsimd)
+        product(3, 0, w2q, xq)
+        v_f(3)
+        add_base(3, nc.gpsimd)
+        v_m(2)
+        v_q(3)
+        a_nqm(3)
+        interleave(s_copy, y_b[0], z[0], 0, HALF)
+        v_m(3)
+        v_e(2)
+        v_e(3)
+        make_y(2)
+        send(2, [nc.sync])
+        make_y(3)
+        send(3, [nc.scalar, nc.sync])
+        yq0 = quantise("yq0", flat3(y_b[0]))
+        store_planes(0, yq0, [nc.sync])
+        interleave(v_copy, y_b[1], z[1], 0, Y_SPLIT)
+        interleave(s_copy, y_b[1], z[1], Y_SPLIT, HALF)
+        yq1 = quantise("yq1", flat3(y_b[1]))
+        store_planes(1, yq1, [nc.sync, nc.scalar])

@@ -48,33 +48,36 @@ def tile_rows_pl_tnrowcentre_kernel(tc, x, w1, w2, gn, dx, og, base, out_0, out_
             nc.sync.dma_start(out=raw[:], in_=src.rearrange("g (p j) c -> (g p) j c", j=PACK))
             return raw
 
-        gn_t = new("gn_t", [P, G, 2])
-        og_t = new("og_t", [P, G, 2])
+        gain_rows = new("gain_rows", [P, P])
+        gain_cols = new("gain_cols", [P, 4, 32])
+        nc.vector.memset(gain_rows[:], 0.0)
         x_raw = load_rows("x_raw", x)
-        nc.scalar.dma_start(out=gn_t[:], in_=gn.rearrange("g (q h) o -> q g (h o)", h=2))
-        nc.scalar.dma_start(out=og_t[:], in_=og.rearrange("g (q h) o -> q g (h o)", h=2))
+        for r, src in enumerate((gn, og)):
+            nc.sync.dma_start(out=gain_rows[r:P:32, :].rearrange("q (i c) -> q i c", c=32),
+                                in_=src.rearrange("g (h q c) o -> q (g h) (c o)", h=2, c=32))
         w1_raw = load_rows("w1_raw", w1)
         dx_raw = load_rows("dx_raw", dx)
         w2_raw = load_rows("w2_raw", w2)
         base_t = []
         for g in range(G):
             t = new("base%d" % g, [P, 2, N])
-            nc.sync.dma_start(out=t[:], in_=base[g].rearrange("(q h) n -> q h n", h=2))
+            nc.sync.dma_start(out=t[:], in_=base[g].rearrange("(h q) n -> q h n", h=2))
             base_t.append(t)
 
         pre = new("pre", [P, 4, 8])
         mean_fac = new("mean_fac", [P, 4, 2])
-        minus_half = new("minus_half", [P, 1])
+        minus_half = new("minus_half", [P, 2])
         nc.gpsimd.memset(minus_half[:], -0.5)
-        nc.gpsimd.memset(pre[:, :, 2], -float(N))
-        nc.gpsimd.memset(mean_fac[:, :, 1], -1.0 / N)
-        gn_f = gn_t[:].rearrange("p g h -> p (g h)")
-        og_f = og_t[:].rearrange("p g h -> p (g h)")
-        nc.gpsimd.tensor_scalar(out=mean_fac[:, :, 0], in0=gn_f, scalar1=1.0, scalar2=0.0, op0=ALU.mult, op1=ALU.add)
-        nc.gpsimd.tensor_scalar(out=pre[:, :, 0], in0=gn_f, scalar1=-float(N), scalar2=0.0, op0=ALU.mult, op1=ALU.add)
-        gain = new("gain", [P, 4])
-        nc.gpsimd.tensor_tensor(out=gain[:], in0=gn_f, in1=og_f, op=ALU.mult)
-        nc.gpsimd.tensor_scalar(out=pre[:, :, 1], in0=gain[:], scalar1=-1.0, scalar2=0.0, op0=ALU.mult, op1=ALU.add)
+        gn_f = gain_cols[:, :, 0]
+        og_f = gain_cols[:, :, 1]
+
+        def v_prep():
+            nc.vector.transpose(out=gain_cols[:].rearrange("p i c -> p (i c)"), in_=gain_rows[:])
+            nc.vector.memset(pre[:, :, 2], -float(N))
+            nc.vector.memset(mean_fac[:, :, 1], -1.0 / N)
+            nc.vector.tensor_copy(out=mean_fac[:, :, 0], in_=gn_f)
+            nc.vector.tensor_scalar(out=pre[:, :, 0], in0=gn_f, scalar1=-float(N), scalar2=None, op0=ALU.mult)
+            nc.vector.scalar_tensor_tensor(out=pre[:, :, 1], in0=gn_f, scalar=-1.0, in1=og_f, op0=ALU.mult, op1=ALU.mult)
 
         def v_copy(out, in_):
             nc.vector.tensor_copy(out=out, in_=in_)
@@ -86,10 +89,6 @@ def tile_rows_pl_tnrowcentre_kernel(tc, x, w1, w2, gn, dx, og, base, out_0, out_
             copy(dst[:, c0:c1, :].rearrange("p (c i) j -> p c j i", i=4),
                  src[:, :, c0:c1].rearrange("p j (c i) -> p c j i", i=4))
 
-        def deal(copy, dst, src, h):
-            copy(dst[:, h].rearrange("p (c i) j -> p c j i", i=2),
-                 src[:].rearrange("p j (c i h) -> p h c j i", i=2, h=2)[:, h])
-
         def quantise(name, flat):
             width = flat.shape[1] // PACK
             codes = new(name + "_codes", [P, width], U32)
@@ -97,47 +96,66 @@ def tile_rows_pl_tnrowcentre_kernel(tc, x, w1, w2, gn, dx, og, base, out_0, out_
             nc.vector.quantize_mx(out=codes[:].bitcast(FP8X4), scales=scales[:], in_=flat)
             return codes, scales
 
+        y_scales = new("y_scales", [P, HALF], U8)
+
+        def quantise_y(g):
+            codes = new("y_codes%d" % g, [P, HALF], U32)
+            nc.vector.quantize_mx(out=codes[:].bitcast(FP8X4), scales=y_scales[4 * g:P, :],
+                                  in_=y_b[g][:].rearrange("p c j -> p (c j)"))
+            return codes
+
         def product(i, bank, wq, xq):
             g, h = divmod(i, 2)
             rows = slice(ROWS * g, ROWS * (g + 1))
-            cols = slice(P * h, P * (h + 1))
-            nc.tensor.matmul_mx(out=banks[g][bank][:], lhsT=wq[0][rows, cols].bitcast(FP8X4), lhsT_scale=wq[1][rows, cols],
+            nc.tensor.matmul_mx(out=banks[g][bank][:], lhsT=wq[h][0][rows, :].bitcast(FP8X4), lhsT_scale=wq[h][1][rows, :],
                                 rhs=xq[0][rows, :].bitcast(FP8X4), rhs_scale=xq[1][rows, :], start=True, stop=True)
 
         x_b = new("x_b", [P, N, PACK], BF16)
         dx_b = new("dx_b", [P, N, PACK], BF16)
-        w1_b = new("w1_b", [P, 2, P, PACK], BF16)
-        w2_b = new("w2_b", [P, 2, P, PACK], BF16)
+        w1_b = new("w1_b", [P, M, PACK], BF16)
+        w2_b = new("w2_b", [P, M, PACK], BF16)
 
         zs, th, sq, q, f, m, e, fb, y = [full(n) for n in ("zs", "th", "sq", "q", "f", "m", "e", "fb", "y")]
         junk_s, junk_v = full("junk_s"), full("junk_v")
-        nmu, ssq, var, rs, r2, cov, kk, qsum, nqm = [
-            col(n) for n in ("nmu", "ssq", "var", "rs", "r2", "cov", "kk", "qsum", "nqm")]
-        fac = [new("fac%d" % i, [P, 4]) for i in range(4)]
-        z = [new("z%d" % g, [P, PACK, HALF]) for g in range(G)]
+        cov, kk, qsum, nqm, r2 = [col(n) for n in ("cov", "kk", "qsum", "nqm", "r2")]
+        nmu, ssq, var, rs = [[new("%s%d" % (n, g), [P, 2]) for g in range(G)] for n in ("nmu", "ssq", "var", "rs")]
+        fac = [new("fac%d" % g, [P, 2, 4]) for g in range(G)]
+
+        def of(tiles, i, j=None):
+            g, h = divmod(i, 2)
+            return tiles[g][:, h:h + 1] if j is None else tiles[g][:, h, j:j + 1]
+
+        z = [new("z%d" % g, [P, PACK, HALF], BF16) for g in range(G)]
+        yr = [new("yr%d" % i, [P, N], BF16) for i in range(4)]
         y_b = [new("y_b%d" % g, [P, HALF, PACK], BF16) for g in range(G)]
 
         def bank_of(i, what):
             g, h = divmod(i, 2)
-            return banks[g][{"z1": h, "tz1": 2 + h, "tz2": 2 * h, "z2": 1 - h}[what]]
+            return banks[g][{"z1": h, "tz1": 2 + h, "tz2": h, "z2": h}[what]]
 
         def a_copy(i):
-            nc.scalar.activation(out=zs[i][:], in_=bank_of(i, "z1")[:], func=ACT.Copy, scale=-1.0 / N, accum_out=nmu[i][:])
+            nc.scalar.activation(out=zs[i][:], in_=bank_of(i, "z1")[:], func=ACT.Copy, scale=-1.0 / N, accum_out=of(nmu, i))
+
+        def a_pre(i):
+            nc.scalar.activation(out=pre[:, i, 3:5], in_=mean_fac[:, i, :], func=ACT.Copy, scale=of(nmu, i))
 
         def a_var(i):
-            nc.scalar.activation(out=junk_s[i][:], in_=zs[i][:], func=ACT.Square, scale=-float(N), bias=nmu[i][:], accum_out=ssq[i][:])
-            nc.scalar.activation(out=pre[:, i, 3:5], in_=mean_fac[:, i, :], func=ACT.Copy, scale=nmu[i][:])
-            nc.scalar.activation(out=var[i][:], in_=ssq[i][:], func=ACT.Copy, scale=1.0 / N, bias=EPS)
+            nc.scalar.activation(out=junk_s[i][:], in_=zs[i][:], func=ACT.Square, scale=-float(N), bias=of(nmu, i), accum_out=of(ssq, i))
 
-        def p_pow(i):
-            nc.gpsimd.tensor_tensor(out=rs[i][:], in0=var[i][:], in1=minus_half[:], op=ALU.pow)
+        def a_eps(g):
+            nc.scalar.activation(out=var[g][:], in_=ssq[g][:], func=ACT.Copy, scale=1.0 / N, bias=EPS)
+
+        def p_pow(g):
+            nc.gpsimd.tensor_tensor(out=rs[g][:], in0=var[g][:], in1=minus_half[:], op=ALU.pow)
 
         def a_fac(i):
-            nc.scalar.activation(out=fac[i][:], in_=pre[:, i, 0:4], func=ACT.Copy, scale=rs[i][:])
-            nc.scalar.activation(out=r2[i][:], in_=fac[i][:, 2:3], func=ACT.Copy, scale=rs[i][:])
+            nc.scalar.activation(out=fac[i // 2][:, i % 2, :], in_=pre[:, i, 0:4], func=ACT.Copy, scale=of(rs, i))
+
+        def a_r2(i):
+            nc.scalar.activation(out=r2[i][:], in_=of(fac, i, 2), func=ACT.Copy, scale=of(rs, i))
 
         def a_tanh(i):
-            nc.scalar.activation(out=th[i][:], in_=zs[i][:], func=ACT.Tanh, scale=fac[i][:, 0:1], bias=fac[i][:, 3:4])
+            nc.scalar.activation(out=th[i][:], in_=zs[i][:], func=ACT.Tanh, scale=of(fac, i, 0), bias=of(fac, i, 3))
 
         def a_sq(i):
             nc.scalar.activation(out=sq[i][:], in_=th[i][:], func=ACT.Square)
@@ -159,7 +177,7 @@ def tile_rows_pl_tnrowcentre_kernel(tc, x, w1, w2, gn, dx, og, base, out_0, out_
 
         def v_f(i):
             g, h = divmod(i, 2)
-            stt(f[i][:], bank_of(i, "tz2")[:], og_t[:, g, h:h + 1], th[i][:], ALU.mult, ALU.mult)
+            stt(f[i][:], bank_of(i, "tz2")[:], gain_cols[:, i, 1:2], th[i][:], ALU.mult, ALU.mult)
 
         def v_m(i):
             stt(m[i][:], sq[i][:], -1.0, bank_of(i, "z2")[:], ALU.add, ALU.mult)
@@ -172,129 +190,158 @@ def tile_rows_pl_tnrowcentre_kernel(tc, x, w1, w2, gn, dx, og, base, out_0, out_
             eng.tensor_tensor(out=fb[i][:], in0=f[i][:], in1=base_t[g][:, h, :], op=ALU.add)
 
         def make_y(i):
-            stt(y[i][:], e[i][:], fac[i][:, 1:2], fb[i][:], ALU.mult, ALU.add)
+            stt(y[i][:], e[i][:], of(fac, i, 1), fb[i][:], ALU.mult, ALU.add)
+
+        def a_round(i):
+            s_copy(yr[i][:], y[i][:])
+
+        def make_yr(i):
+            stt(yr[i][:], e[i][:], of(fac, i, 1), fb[i][:], ALU.mult, ALU.add)
 
         def send(i, queues):
             g, h = divmod(i, 2)
-            k = 0
-            for a in range(2):
-                for b in range(2):
-                    queues[k % len(queues)].dma_start(out=z[g][ROWS * b:ROWS * (b + 1), 2 * a + h, :],
-                                                      in_=y[i][a:P:2, HALF * b:HALF * (b + 1)])
-                    k = k + 1
-            nc.sync.dma_start(out=out_0[M * g:M * (g + 1), :].rearrange("(q h) n -> q h n", h=2)[:, h, :], in_=y[i][:])
+            for b in range(2):
+                queues[b % len(queues)].dma_start(
+                    out=z[g][ROWS * b + 32 * h:ROWS * b + 32 * (h + 1)],
+                    in_=yr[i][:, HALF * b:HALF * (b + 1)])
 
-        def store_planes(g, yq, queues):
-            codes, scales = yq
+        def store_y(i):
+            g, h = divmod(i, 2)
+            nc.sync.dma_start(out=out_0[P * i:P * (i + 1), :], in_=y[i][:])
+
+        def store_words(g, codes, queues):
             words = out_1.rearrange("s p n u -> (s p) (n u)").bitcast(I32)
-            bytes4 = out_2.rearrange("s f n -> (s f) n").bitcast(I32)
             for b in range(2):
                 queues[b % len(queues)].dma_start(out=words[ROWS * g:ROWS * (g + 1), HALF * b:HALF * (b + 1)],
                                                   in_=codes[ROWS * b:ROWS * (b + 1), :].bitcast(I32))
+
+        def store_scales(queues):
+            bytes4 = out_2.bitcast(I32).rearrange("s (g lo r) n -> (s lo) g r n", g=G, r=4)
             for quad in range(4):
                 b, lo = divmod(quad, 2)
-                f0 = 8 * g + 4 * lo
-                queues[quad % len(queues)].dma_start(out=bytes4[f0:f0 + 4, (HALF // 4) * b:(HALF // 4) * (b + 1)],
-                                                     in_=scales[32 * quad:32 * quad + 4, :].bitcast(I32))
+                queues[quad % len(queues)].dma_start(out=bytes4[lo, :, :, (HALF // 4) * b:(HALF // 4) * (b + 1)],
+                                                     in_=y_scales[32 * quad:32 * quad + 8, :].bitcast(I32))
 
         def flat3(t):
             return t[:].rearrange("p c j -> p (c j)")
 
-        def flat4(t):
-            return t[:].rearrange("p h c j -> p (h c j)")
+        def flat4(t, h):
+            return t[:, P * h:P * (h + 1), :].rearrange("p c j -> p (c j)")
+
+        def halves(pair):
+            return [(pair[0][:, P * h:P * (h + 1)], pair[1][:, P * h:P * (h + 1)]) for h in range(2)]
 
         interleave(v_copy, x_b, x_raw, 0, X_SPLIT)
         interleave(s_copy, x_b, x_raw, X_SPLIT, N)
         xq = quantise("xq", flat3(x_b))
-        deal(s_copy, w1_b, w1_raw, 0)
-        deal(v_copy, w1_b, w1_raw, 1)
-        w1q = quantise("w1q", flat4(w1_b))
-        for i in (0, 2, 1, 3):
-            product(i, i % 2, w1q, xq)
-        a_copy(0)
-        interleave(v_copy, dx_b, dx_raw, 0, DX_SPLIT)
-        interleave(s_copy, dx_b, dx_raw, DX_SPLIT, N)
+        interleave(s_copy, w1_b, w1_raw, 0, P)
+        w1q = [quantise("w1q0", flat4(w1_b, 0))]
+        product(0, 0, w1q, xq)
+        interleave(v_copy, w1_b, w1_raw, P, M)
+        w1q.append(quantise("w1q1", flat4(w1_b, 1)))
+        product(1, 1, w1q, xq)
+        product(2, 0, w1q, xq)
+        product(3, 1, w1q, xq)
+        v_prep()
+        interleave(v_copy, dx_b, dx_raw, 0, N)
         dxq = quantise("dxq", flat3(dx_b))
-        for i in (0, 2, 1, 3):
+        for i in range(4):
             product(i, 2 + i % 2, w1q, dxq)
-        a_var(0)
-        p_pow(0)
-        a_copy(1)
-        a_var(1)
-        p_pow(1)
-        deal(v_copy, w2_b, w2_raw, 0)
-        deal(v_copy, w2_b, w2_raw, 1)
-        v_cov(0)
-        w2q = quantise("w2q", flat4(w2_b))
+        a_copy(0)
+        interleave(v_copy, w2_b, w2_raw, 0, M)
+        w2q = halves(quantise("w2q", flat3(w2_b)))
         product(0, 0, w2q, dxq)
-        product(0, 1, w2q, xq)
-        a_fac(0)
-        a_kk(0)
-        a_tanh(0)
+        a_copy(1)
+        product(1, 1, w2q, dxq)
+        a_var(0)
+        a_var(1)
+        a_eps(0)
+        p_pow(0)
+        a_pre(0)
+        v_cov(0)
+        a_pre(1)
         v_cov(1)
-        v_q(0)
-        product(1, 2, w2q, dxq)
-        a_fac(1)
-        a_kk(1)
-        a_sq(0)
-        a_nqm(0)
-        v_f(0)
-        add_base(0, nc.gpsimd)
         a_copy(2)
-        a_var(2)
-        p_pow(2)
-        product(1, 0, w2q, xq)
         product(2, 0, w2q, dxq)
-        v_m(0)
-        v_q(1)
-        v_e(0)
-        v_cov(2)
-        make_y(0)
-        send(0, [nc.sync])
-        a_nqm(1)
-        a_tanh(1)
-        a_sq(1)
-        a_fac(2)
-        a_kk(2)
-        v_f(1)
-        add_base(1, nc.gpsimd)
         a_copy(3)
-        a_var(3)
-        p_pow(3)
-        product(2, 1, w2q, xq)
+        product(3, 1, w2q, dxq)
+        a_fac(0)
+        a_fac(1)
+        a_tanh(0)
+        v_f(0)
+        product(0, 0, w2q, xq)
+        add_base(0, nc.gpsimd)
+        a_r2(0)
+        a_r2(1)
+        a_kk(0)
+        v_q(0)
+        a_tanh(1)
+        v_f(1)
+        product(1, 1, w2q, xq)
+        add_base(1, nc.gpsimd)
+        a_kk(1)
+        v_q(1)
+        a_pre(2)
+        a_pre(3)
+        a_sq(0)
+        v_m(0)
+        a_sq(1)
         v_m(1)
-        v_q(2)
-        product(3, 2, w2q, dxq)
-        v_e(1)
+        a_var(2)
+        v_cov(2)
+        a_var(3)
         v_cov(3)
-        make_y(1)
-        send(1, [nc.sync])
-        a_tanh(2)
-        a_nqm(2)
-        a_sq(2)
+        a_eps(1)
+        p_pow(1)
+        a_nqm(0)
+        v_e(0)
+        a_nqm(1)
+        v_e(1)
+        a_fac(2)
+        make_y(0)
+        store_y(0)
         a_fac(3)
-        a_kk(3)
-        a_tanh(3)
-        a_sq(3)
+        make_y(1)
+        store_y(1)
+        a_tanh(2)
         v_f(2)
+        product(2, 0, w2q, xq)
         add_base(2, nc.gpsimd)
-        product(3, 0, w2q, xq)
+        a_r2(2)
+        a_r2(3)
+        a_kk(2)
+        v_q(2)
+        a_tanh(3)
         v_f(3)
+        product(3, 1, w2q, xq)
         add_base(3, nc.gpsimd)
-        v_m(2)
+        a_kk(3)
         v_q(3)
-        a_nqm(3)
-        interleave(s_copy, y_b[0], z[0], 0, HALF)
+        a_round(0)
+        send(0, [nc.sync])
+        a_round(1)
+        send(1, [nc.sync])
+        a_sq(2)
+        v_m(2)
+        a_sq(3)
         v_m(3)
+        a_nqm(2)
         v_e(2)
+        a_nqm(3)
         v_e(3)
-        make_y(2)
-        send(2, [nc.sync])
-        make_y(3)
-        send(3, [nc.scalar, nc.sync])
-        yq0 = quantise("yq0", flat3(y_b[0]))
-        store_planes(0, yq0, [nc.sync])
-        interleave(v_copy, y_b[1], z[1], 0, Y_SPLIT)
+        interleave(s_copy, y_b[0], z[0], 0, HALF)
+        make_yr(2)
+        send(2, [nc.sync, nc.scalar])
+        make_yr(3)
+        send(3, [nc.sync, nc.scalar])
         interleave(s_copy, y_b[1], z[1], Y_SPLIT, HALF)
-        yq1 = quantise("yq1", flat3(y_b[1]))
-        store_planes(1, yq1, [nc.sync, nc.scalar])
+        make_y(2)
+        store_y(2)
+        make_y(3)
+        store_y(3)
+        yc0 = quantise_y(0)
+        store_words(0, yc0, [nc.sync])
+        interleave(v_copy, y_b[1], z[1], 0, Y_SPLIT)
+        yc1 = quantise_y(1)
+        store_words(1, yc1, [nc.sync, nc.scalar])
+        store_scales([nc.sync, nc.scalar])

@@ -16,11 +16,12 @@ ACT = mybir.ActivationFunctionType
 
 P = 128
 ROWS = 64
+QUAD = 32
 PACK = 4
+TILES = G * M // P
 HALF = N // 2
 EPS = 0.05
 X_SPLIT = 352
-DX_SPLIT = 384
 Y_SPLIT = 176
 
 
@@ -34,314 +35,245 @@ def tile_rows_pl_tnrowcentre_kernel(tc, x, w1, w2, gn, dx, og, base, out_0, out_
         def new(name, shape, dtype=F32):
             return sb.tile(shape, dtype, name=name, align_bytes=64)
 
-        def col(name):
-            return [new("%s%d" % (name, i), [P, 1]) for i in range(4)]
+        def per_tile(name, width, dtype=F32):
+            return [new("%s%d" % (name, i), [P, width], dtype) for i in range(TILES)]
 
-        def full(name):
-            return [new("%s%d" % (name, i), [P, N]) for i in range(4)]
+        def per_group(name, shape, dtype=F32):
+            return [new("%s%d" % (name, g), shape, dtype) for g in range(G)]
 
-        banks = [[ps.tile([P, N], F32, name="bank%d%d" % (g, b)) for b in range(4)] for g in range(G)]
+        def tiles_of(g):
+            return (2 * g, 2 * g + 1)
 
-        def load_rows(name, src):
-            width = src.shape[2]
-            raw = new(name, [P, PACK, width])
+        def column(group_tiles, i):
+            return group_tiles[i // 2][:, i % 2:i % 2 + 1]
+
+        def load_operand(name, src):
+            raw = new(name, [P, PACK, src.shape[2]])
             nc.sync.dma_start(out=raw[:], in_=src.rearrange("g (p j) c -> (g p) j c", j=PACK))
             return raw
 
-        gain_rows = new("gain_rows", [P, P])
-        gain_cols = new("gain_cols", [P, 4, 32])
+        x_raw = load_operand("x_raw", x)
+        w1_raw = load_operand("w1_raw", w1)
+        gain_rows = new("gain_rows", [P, TILES * QUAD])
         nc.vector.memset(gain_rows[:], 0.0)
-        x_raw = load_rows("x_raw", x)
         for r, src in enumerate((gn, og)):
-            nc.sync.dma_start(out=gain_rows[r:P:32, :].rearrange("q (i c) -> q i c", c=32),
-                                in_=src.rearrange("g (h q c) o -> q (g h) (c o)", h=2, c=32))
-        w1_raw = load_rows("w1_raw", w1)
-        dx_raw = load_rows("dx_raw", dx)
-        w2_raw = load_rows("w2_raw", w2)
-        base_t = []
+            nc.sync.dma_start(out=gain_rows[r:P:QUAD, :].rearrange("q (i c) -> q i c", c=QUAD),
+                              in_=src.rearrange("g (h q c) o -> q (g h) (c o)", h=2, c=QUAD))
+        dx_raw = load_operand("dx_raw", dx)
+        w2_raw = load_operand("w2_raw", w2)
+        base_t = per_group("base", [P, 2, N])
         for g in range(G):
-            t = new("base%d" % g, [P, 2, N])
-            nc.sync.dma_start(out=t[:], in_=base[g].rearrange("(h q) n -> q h n", h=2))
-            base_t.append(t)
+            nc.sync.dma_start(out=base_t[g][:], in_=base[g].rearrange("(h q) n -> q h n", h=2))
 
-        pre = new("pre", [P, 4, 8])
-        mean_fac = new("mean_fac", [P, 4, 2])
-        minus_half = new("minus_half", [P, 2])
-        nc.gpsimd.memset(minus_half[:], -0.5)
-        gn_f = gain_cols[:, :, 0]
-        og_f = gain_cols[:, :, 1]
-
-        def v_prep():
-            nc.vector.transpose(out=gain_cols[:].rearrange("p i c -> p (i c)"), in_=gain_rows[:])
-            nc.vector.memset(pre[:, :, 2], -float(N))
-            nc.vector.memset(mean_fac[:, :, 1], -1.0 / N)
-            nc.vector.tensor_copy(out=mean_fac[:, :, 0], in_=gn_f)
-            nc.vector.tensor_scalar(out=pre[:, :, 0], in0=gn_f, scalar1=-float(N), scalar2=None, op0=ALU.mult)
-            nc.vector.scalar_tensor_tensor(out=pre[:, :, 1], in0=gn_f, scalar=-1.0, in1=og_f, op0=ALU.mult, op1=ALU.mult)
-
-        def v_copy(out, in_):
+        def on_vector(out, in_):
             nc.vector.tensor_copy(out=out, in_=in_)
 
-        def s_copy(out, in_):
+        def on_scalar(out, in_):
             nc.scalar.activation(out=out, in_=in_, func=ACT.Copy)
 
         def interleave(copy, dst, src, c0, c1):
             copy(dst[:, c0:c1, :].rearrange("p (c i) j -> p c j i", i=4),
                  src[:, :, c0:c1].rearrange("p j (c i) -> p c j i", i=4))
 
-        def quantise(name, flat):
-            width = flat.shape[1] // PACK
-            codes = new(name + "_codes", [P, width], U32)
-            scales = new(name + "_scales", [P, width], U8)
-            nc.vector.quantize_mx(out=codes[:].bitcast(FP8X4), scales=scales[:], in_=flat)
+        def quantise(name, grouped, c0, c1):
+            codes = new(name + "_codes", [P, c1 - c0], U32)
+            scales = new(name + "_scales", [P, c1 - c0], U8)
+            nc.vector.quantize_mx(out=codes[:].bitcast(FP8X4), scales=scales[:],
+                                  in_=grouped[:, c0:c1, :].rearrange("p c j -> p (c j)"))
             return codes, scales
 
+        banks = [[ps.tile([P, N], F32, name="bank%d%d" % (g, k)) for k in range(4)] for g in range(G)]
+        z_bank = [banks[i // 2][i % 2] for i in range(TILES)]
+        tz1_bank = [banks[i // 2][2 + i % 2] for i in range(TILES)]
+
+        def product(i, bank, weights, moving):
+            rows = slice(ROWS * (i // 2), ROWS * (i // 2 + 1))
+            codes, scales = weights[i % 2]
+            nc.tensor.matmul_mx(out=bank[:], lhsT=codes[rows, :].bitcast(FP8X4), lhsT_scale=scales[rows, :],
+                                rhs=moving[0][rows, :].bitcast(FP8X4), rhs_scale=moving[1][rows, :],
+                                start=True, stop=True)
+
+        x_b, dx_b = new("x_b", [P, N, PACK], BF16), new("dx_b", [P, N, PACK], BF16)
+        w1_b, w2_b = new("w1_b", [P, M, PACK], BF16), new("w2_b", [P, M, PACK], BF16)
+
+        interleave(on_vector, x_b, x_raw, 0, X_SPLIT)
+        interleave(on_scalar, x_b, x_raw, X_SPLIT, N)
+        xq = quantise("xq", x_b, 0, N)
+        interleave(on_scalar, w1_b, w1_raw, 0, P)
+        w1q = [quantise("w1q0", w1_b, 0, P)]
+        product(0, z_bank[0], w1q, xq)
+        interleave(on_vector, w1_b, w1_raw, P, M)
+        w1q.append(quantise("w1q1", w1_b, P, M))
+        for i in range(1, TILES):
+            product(i, z_bank[i], w1q, xq)
+
+        gains = new("gains", [P, TILES, QUAD])
+        by_root = new("by_root", [P, TILES, 8])
+        by_mean = new("by_mean", [P, TILES, 2])
+        minus_half = new("minus_half", [P, 2])
+        nc.gpsimd.memset(minus_half[:], -0.5)
+        nc.vector.transpose(out=gains[:].rearrange("p i c -> p (i c)"), in_=gain_rows[:])
+        nc.vector.memset(by_root[:, :, 2], -float(N))
+        nc.vector.memset(by_mean[:, :, 1], -1.0 / N)
+        nc.vector.tensor_copy(out=by_mean[:, :, 0], in_=gains[:, :, 0])
+        nc.vector.tensor_scalar(out=by_root[:, :, 0], in0=gains[:, :, 0], scalar1=-float(N), scalar2=None,
+                                op0=ALU.mult)
+        nc.vector.scalar_tensor_tensor(out=by_root[:, :, 1], in0=gains[:, :, 0], scalar=-1.0, in1=gains[:, :, 1],
+                                       op0=ALU.mult, op1=ALU.mult)
+
+        interleave(on_vector, dx_b, dx_raw, 0, N)
+        dxq = quantise("dxq", dx_b, 0, N)
+        for i in tiles_of(0):
+            product(i, tz1_bank[i], w1q, dxq)
+
+        zs, th, th_sq, q, gated, sech_z2, change, gated_base, y = [
+            per_tile(name, N) for name in ("zs", "th", "th_sq", "q", "gated", "sech_z2", "change", "gated_base", "y")]
+        squares, cov_terms = per_tile("squares", N), per_tile("cov_terms", N)
+        cov, slope, q_sum, minus_q_mean, slope_fac = [
+            per_tile(name, 1) for name in ("cov", "slope", "q_sum", "minus_q_mean", "slope_fac")]
+        minus_mu, square_sum, variance, root = [
+            per_group(name, [P, 2]) for name in ("minus_mu", "square_sum", "variance", "root")]
+        rooted = per_tile("rooted", 4)
+        y_round = per_tile("y_round", N, BF16)
+        y_rows = per_group("y_rows", [P, PACK, HALF], BF16)
+        y_b = per_group("y_b", [P, HALF, PACK], BF16)
+        y_codes = per_group("y_codes", [P, HALF], U32)
         y_scales = new("y_scales", [P, HALF], U8)
 
-        def quantise_y(g):
-            codes = new("y_codes%d" % g, [P, HALF], U32)
-            nc.vector.quantize_mx(out=codes[:].bitcast(FP8X4), scales=y_scales[4 * g:P, :],
-                                  in_=y_b[g][:].rearrange("p c j -> p (c j)"))
-            return codes
+        def scaled(out, in_, scale):
+            nc.scalar.activation(out=out, in_=in_, func=ACT.Copy, scale=scale)
 
-        def product(i, bank, wq, xq):
-            g, h = divmod(i, 2)
-            rows = slice(ROWS * g, ROWS * (g + 1))
-            nc.tensor.matmul_mx(out=banks[g][bank][:], lhsT=wq[h][0][rows, :].bitcast(FP8X4), lhsT_scale=wq[h][1][rows, :],
-                                rhs=xq[0][rows, :].bitcast(FP8X4), rhs_scale=xq[1][rows, :], start=True, stop=True)
+        def fused(out, in0, scalar, in1, op0, op1, accum_out=None):
+            nc.vector.scalar_tensor_tensor(out=out, in0=in0, scalar=scalar, in1=in1, op0=op0, op1=op1,
+                                           accum_out=accum_out)
 
-        x_b = new("x_b", [P, N, PACK], BF16)
-        dx_b = new("dx_b", [P, N, PACK], BF16)
-        w1_b = new("w1_b", [P, M, PACK], BF16)
-        w2_b = new("w2_b", [P, M, PACK], BF16)
+        def copy_z1(g):
+            for i in tiles_of(g):
+                nc.scalar.activation(out=zs[i][:], in_=z_bank[i][:], func=ACT.Copy, scale=-1.0 / N,
+                                     accum_out=column(minus_mu, i))
 
-        zs, th, sq, q, f, m, e, fb, y = [full(n) for n in ("zs", "th", "sq", "q", "f", "m", "e", "fb", "y")]
-        junk_s, junk_v = full("junk_s"), full("junk_v")
-        cov, kk, qsum, nqm, r2 = [col(n) for n in ("cov", "kk", "qsum", "nqm", "r2")]
-        nmu, ssq, var, rs = [[new("%s%d" % (n, g), [P, 2]) for g in range(G)] for n in ("nmu", "ssq", "var", "rs")]
-        fac = [new("fac%d" % g, [P, 2, 4]) for g in range(G)]
+        def spread(g):
+            for i in tiles_of(g):
+                nc.scalar.activation(out=squares[i][:], in_=zs[i][:], func=ACT.Square, scale=-float(N),
+                                     bias=column(minus_mu, i), accum_out=column(square_sum, i))
+            nc.scalar.activation(out=variance[g][:], in_=square_sum[g][:], func=ACT.Copy, scale=1.0 / N, bias=EPS)
+            nc.gpsimd.tensor_tensor(out=root[g][:], in0=variance[g][:], in1=minus_half[:], op=ALU.pow)
 
-        def of(tiles, i, j=None):
-            g, h = divmod(i, 2)
-            return tiles[g][:, h:h + 1] if j is None else tiles[g][:, h, j:j + 1]
+        def mean_terms(g):
+            for i in tiles_of(g):
+                scaled(by_root[:, i, 3:5], by_mean[:, i, :], column(minus_mu, i))
 
-        z = [new("z%d" % g, [P, PACK, HALF], BF16) for g in range(G)]
-        yr = [new("yr%d" % i, [P, N], BF16) for i in range(4)]
-        y_b = [new("y_b%d" % g, [P, HALF, PACK], BF16) for g in range(G)]
+        def covariance(g):
+            for i in tiles_of(g):
+                fused(cov_terms[i][:], zs[i][:], by_root[:, i, 4:5], tz1_bank[i][:], ALU.add, ALU.mult, cov[i][:])
 
-        def bank_of(i, what):
-            g, h = divmod(i, 2)
-            return banks[g][{"z1": h, "tz1": 2 + h, "tz2": h, "z2": h}[what]]
+        def tanh(i):
+            nc.scalar.activation(out=th[i][:], in_=zs[i][:], func=ACT.Tanh, scale=rooted[i][:, 0:1],
+                                 bias=rooted[i][:, 3:4])
 
-        def a_copy(i):
-            nc.scalar.activation(out=zs[i][:], in_=bank_of(i, "z1")[:], func=ACT.Copy, scale=-1.0 / N, accum_out=of(nmu, i))
+        def tanh_and_slope(g):
+            first, second = tiles_of(g)
+            for i in tiles_of(g):
+                scaled(rooted[i][:], by_root[:, i, 0:4], column(root, i))
+            tanh(first)
+            for i in tiles_of(g):
+                scaled(slope_fac[i][:], rooted[i][:, 2:3], column(root, i))
+            scaled(slope[first][:], cov[first][:], slope_fac[first][:])
+            tanh(second)
+            scaled(slope[second][:], cov[second][:], slope_fac[second][:])
 
-        def a_pre(i):
-            nc.scalar.activation(out=pre[:, i, 3:5], in_=mean_fac[:, i, :], func=ACT.Copy, scale=of(nmu, i))
+        def square_tanh(g):
+            for i in tiles_of(g):
+                nc.scalar.activation(out=th_sq[i][:], in_=th[i][:], func=ACT.Square)
 
-        def a_var(i):
-            nc.scalar.activation(out=junk_s[i][:], in_=zs[i][:], func=ACT.Square, scale=-float(N), bias=of(nmu, i), accum_out=of(ssq, i))
+        def empty_banks(g, w2q):
+            for i in tiles_of(g):
+                fused(gated[i][:], z_bank[i][:], gains[:, i, 1:2], th[i][:], ALU.mult, ALU.mult)
+                product(i, z_bank[i], w2q, xq)
+                nc.gpsimd.tensor_tensor(out=gated_base[i][:], in0=gated[i][:], in1=base_t[g][:, i % 2, :], op=ALU.add)
+                fused(q[i][:], zs[i][:], slope[i][:], tz1_bank[i][:], ALU.mult, ALU.add, q_sum[i][:])
+            for i in tiles_of(g):
+                fused(sech_z2[i][:], th_sq[i][:], -1.0, z_bank[i][:], ALU.add, ALU.mult)
 
-        def a_eps(g):
-            nc.scalar.activation(out=var[g][:], in_=ssq[g][:], func=ACT.Copy, scale=1.0 / N, bias=EPS)
+        def q_means(g):
+            for i in tiles_of(g):
+                scaled(minus_q_mean[i][:], q_sum[i][:], -1.0 / N)
 
-        def p_pow(g):
-            nc.gpsimd.tensor_tensor(out=rs[g][:], in0=var[g][:], in1=minus_half[:], op=ALU.pow)
+        def changes(g):
+            for i in tiles_of(g):
+                fused(change[i][:], q[i][:], minus_q_mean[i][:], sech_z2[i][:], ALU.add, ALU.mult)
 
-        def a_fac(i):
-            nc.scalar.activation(out=fac[i // 2][:, i % 2, :], in_=pre[:, i, 0:4], func=ACT.Copy, scale=of(rs, i))
+        def result(i, out):
+            fused(out[:], change[i][:], rooted[i][:, 1:2], gated_base[i][:], ALU.mult, ALU.add)
 
-        def a_r2(i):
-            nc.scalar.activation(out=r2[i][:], in_=of(fac, i, 2), func=ACT.Copy, scale=of(rs, i))
-
-        def a_tanh(i):
-            nc.scalar.activation(out=th[i][:], in_=zs[i][:], func=ACT.Tanh, scale=of(fac, i, 0), bias=of(fac, i, 3))
-
-        def a_sq(i):
-            nc.scalar.activation(out=sq[i][:], in_=th[i][:], func=ACT.Square)
-
-        def a_kk(i):
-            nc.scalar.activation(out=kk[i][:], in_=cov[i][:], func=ACT.Copy, scale=r2[i][:])
-
-        def a_nqm(i):
-            nc.scalar.activation(out=nqm[i][:], in_=qsum[i][:], func=ACT.Copy, scale=-1.0 / N)
-
-        def stt(out, in0, scalar, in1, op0, op1, accum_out=None):
-            nc.vector.scalar_tensor_tensor(out=out, in0=in0, scalar=scalar, in1=in1, op0=op0, op1=op1, accum_out=accum_out)
-
-        def v_cov(i):
-            stt(junk_v[i][:], zs[i][:], pre[:, i, 4:5], bank_of(i, "tz1")[:], ALU.add, ALU.mult, cov[i][:])
-
-        def v_q(i):
-            stt(q[i][:], zs[i][:], kk[i][:], bank_of(i, "tz1")[:], ALU.mult, ALU.add, qsum[i][:])
-
-        def v_f(i):
-            g, h = divmod(i, 2)
-            stt(f[i][:], bank_of(i, "tz2")[:], gain_cols[:, i, 1:2], th[i][:], ALU.mult, ALU.mult)
-
-        def v_m(i):
-            stt(m[i][:], sq[i][:], -1.0, bank_of(i, "z2")[:], ALU.add, ALU.mult)
-
-        def v_e(i):
-            stt(e[i][:], q[i][:], nqm[i][:], m[i][:], ALU.add, ALU.mult)
-
-        def add_base(i, eng):
-            g, h = divmod(i, 2)
-            eng.tensor_tensor(out=fb[i][:], in0=f[i][:], in1=base_t[g][:, h, :], op=ALU.add)
-
-        def make_y(i):
-            stt(y[i][:], e[i][:], of(fac, i, 1), fb[i][:], ALU.mult, ALU.add)
-
-        def a_round(i):
-            s_copy(yr[i][:], y[i][:])
-
-        def make_yr(i):
-            stt(yr[i][:], e[i][:], of(fac, i, 1), fb[i][:], ALU.mult, ALU.add)
-
-        def send(i, queues):
-            g, h = divmod(i, 2)
-            for b in range(2):
-                queues[b % len(queues)].dma_start(
-                    out=z[g][ROWS * b + 32 * h:ROWS * b + 32 * (h + 1)],
-                    in_=yr[i][:, HALF * b:HALF * (b + 1)])
-
-        def store_y(i):
-            g, h = divmod(i, 2)
+        def store_result(i):
             nc.sync.dma_start(out=out_0[P * i:P * (i + 1), :], in_=y[i][:])
 
-        def store_words(g, codes, queues):
+        def regroup(i, queues):
+            for b in range(2):
+                first = ROWS * b + QUAD * (i % 2)
+                queues[b].dma_start(out=y_rows[i // 2][first:first + QUAD], in_=y_round[i][:, HALF * b:HALF * (b + 1)])
+
+        def quantise_result(g, queues):
+            nc.vector.quantize_mx(out=y_codes[g][:].bitcast(FP8X4), scales=y_scales[PACK * g:P, :],
+                                  in_=y_b[g][:].rearrange("p c j -> p (c j)"))
             words = out_1.rearrange("s p n u -> (s p) (n u)").bitcast(I32)
             for b in range(2):
-                queues[b % len(queues)].dma_start(out=words[ROWS * g:ROWS * (g + 1), HALF * b:HALF * (b + 1)],
-                                                  in_=codes[ROWS * b:ROWS * (b + 1), :].bitcast(I32))
+                queues[b].dma_start(out=words[ROWS * g:ROWS * (g + 1), HALF * b:HALF * (b + 1)],
+                                    in_=y_codes[g][ROWS * b:ROWS * (b + 1), :].bitcast(I32))
 
         def store_scales(queues):
-            bytes4 = out_2.bitcast(I32).rearrange("s (g lo r) n -> (s lo) g r n", g=G, r=4)
-            for quad in range(4):
+            rows = out_2.bitcast(I32).rearrange("s (g lo r) (b c) -> (s lo) b g r c", g=G, r=PACK, b=2)
+            for quad in range(P // QUAD):
                 b, lo = divmod(quad, 2)
-                queues[quad % len(queues)].dma_start(out=bytes4[lo, :, :, (HALF // 4) * b:(HALF // 4) * (b + 1)],
-                                                     in_=y_scales[32 * quad:32 * quad + 8, :].bitcast(I32))
+                queues[lo].dma_start(out=rows[lo, b],
+                                     in_=y_scales[QUAD * quad:QUAD * quad + G * PACK, :].bitcast(I32))
 
-        def flat3(t):
-            return t[:].rearrange("p c j -> p (c j)")
+        one_queue, both_queues = (nc.sync, nc.sync), (nc.sync, nc.scalar)
+        copy_z1(0)
+        spread(0)
+        mean_terms(0)
+        copy_z1(1)
+        interleave(on_vector, w2_b, w2_raw, 0, M)
+        w2_codes, w2_scales = quantise("w2q", w2_b, 0, M)
+        w2q = [(w2_codes[:, P * h:P * (h + 1)], w2_scales[:, P * h:P * (h + 1)]) for h in range(2)]
+        for i in tiles_of(0):
+            product(i, z_bank[i], w2q, dxq)
+        for i in tiles_of(1):
+            product(i, tz1_bank[i], w1q, dxq)
+        for i in tiles_of(1):
+            product(i, z_bank[i], w2q, dxq)
+        covariance(0)
+        tanh_and_slope(0)
+        mean_terms(1)
+        square_tanh(0)
+        empty_banks(0, w2q)
+        spread(1)
+        q_means(0)
+        covariance(1)
+        tanh_and_slope(1)
 
-        def flat4(t, h):
-            return t[:, P * h:P * (h + 1), :].rearrange("p c j -> p (c j)")
+        changes(0)
+        for i in tiles_of(0):
+            result(i, y[i])
+            store_result(i)
+        for i in tiles_of(0):
+            on_scalar(y_round[i][:], y[i][:])
+            regroup(i, one_queue)
 
-        def halves(pair):
-            return [(pair[0][:, P * h:P * (h + 1)], pair[1][:, P * h:P * (h + 1)]) for h in range(2)]
-
-        interleave(v_copy, x_b, x_raw, 0, X_SPLIT)
-        interleave(s_copy, x_b, x_raw, X_SPLIT, N)
-        xq = quantise("xq", flat3(x_b))
-        interleave(s_copy, w1_b, w1_raw, 0, P)
-        w1q = [quantise("w1q0", flat4(w1_b, 0))]
-        product(0, 0, w1q, xq)
-        interleave(v_copy, w1_b, w1_raw, P, M)
-        w1q.append(quantise("w1q1", flat4(w1_b, 1)))
-        product(1, 1, w1q, xq)
-        product(2, 0, w1q, xq)
-        product(3, 1, w1q, xq)
-        v_prep()
-        interleave(v_copy, dx_b, dx_raw, 0, N)
-        dxq = quantise("dxq", flat3(dx_b))
-        for i in range(4):
-            product(i, 2 + i % 2, w1q, dxq)
-        a_copy(0)
-        interleave(v_copy, w2_b, w2_raw, 0, M)
-        w2q = halves(quantise("w2q", flat3(w2_b)))
-        product(0, 0, w2q, dxq)
-        a_copy(1)
-        product(1, 1, w2q, dxq)
-        a_var(0)
-        a_var(1)
-        a_eps(0)
-        p_pow(0)
-        a_pre(0)
-        v_cov(0)
-        a_pre(1)
-        v_cov(1)
-        a_copy(2)
-        product(2, 0, w2q, dxq)
-        a_copy(3)
-        product(3, 1, w2q, dxq)
-        a_fac(0)
-        a_fac(1)
-        a_tanh(0)
-        v_f(0)
-        product(0, 0, w2q, xq)
-        add_base(0, nc.gpsimd)
-        a_r2(0)
-        a_r2(1)
-        a_kk(0)
-        v_q(0)
-        a_tanh(1)
-        v_f(1)
-        product(1, 1, w2q, xq)
-        add_base(1, nc.gpsimd)
-        a_kk(1)
-        v_q(1)
-        a_pre(2)
-        a_pre(3)
-        a_sq(0)
-        v_m(0)
-        a_sq(1)
-        v_m(1)
-        a_var(2)
-        v_cov(2)
-        a_var(3)
-        v_cov(3)
-        a_eps(1)
-        p_pow(1)
-        a_nqm(0)
-        v_e(0)
-        a_nqm(1)
-        v_e(1)
-        a_fac(2)
-        make_y(0)
-        store_y(0)
-        a_fac(3)
-        make_y(1)
-        store_y(1)
-        a_tanh(2)
-        v_f(2)
-        product(2, 0, w2q, xq)
-        add_base(2, nc.gpsimd)
-        a_r2(2)
-        a_r2(3)
-        a_kk(2)
-        v_q(2)
-        a_tanh(3)
-        v_f(3)
-        product(3, 1, w2q, xq)
-        add_base(3, nc.gpsimd)
-        a_kk(3)
-        v_q(3)
-        a_round(0)
-        send(0, [nc.sync])
-        a_round(1)
-        send(1, [nc.sync])
-        a_sq(2)
-        v_m(2)
-        a_sq(3)
-        v_m(3)
-        a_nqm(2)
-        v_e(2)
-        a_nqm(3)
-        v_e(3)
-        interleave(s_copy, y_b[0], z[0], 0, HALF)
-        make_yr(2)
-        send(2, [nc.sync, nc.scalar])
-        make_yr(3)
-        send(3, [nc.sync, nc.scalar])
-        interleave(s_copy, y_b[1], z[1], Y_SPLIT, HALF)
-        make_y(2)
-        store_y(2)
-        make_y(3)
-        store_y(3)
-        yc0 = quantise_y(0)
-        store_words(0, yc0, [nc.sync])
-        interleave(v_copy, y_b[1], z[1], 0, Y_SPLIT)
-        yc1 = quantise_y(1)
-        store_words(1, yc1, [nc.sync, nc.scalar])
-        store_scales([nc.sync, nc.scalar])
+        square_tanh(1)
+        empty_banks(1, w2q)
+        q_means(1)
+        changes(1)
+        for i in tiles_of(1):
+            result(i, y_round[i])
+            regroup(i, both_queues)
+        for i in tiles_of(1):
+            result(i, y[i])
+            store_result(i)
+        interleave(on_scalar, y_b[0], y_rows[0], 0, HALF)
+        quantise_result(0, one_queue)
+        interleave(on_vector, y_b[1], y_rows[1], 0, Y_SPLIT)
+        interleave(on_scalar, y_b[1], y_rows[1], Y_SPLIT, HALF)
+        quantise_result(1, both_queues)
+        store_scales(both_queues)

@@ -188,7 +188,7 @@ def tile_rows_pl_tnrowcentre_kernel(tc, x, w1, w2, gn, dx, og, base, out_0, out_
 
         def empty_banks(g, w2q):
             for i in tiles_of(g):
-                fused(gated[i][:], z_bank[i][:], gains[:, i, 1:2], th[i][:], ALU.mult, ALU.mult)
+                fused(gated[i][:], th[i][:], gains[:, i, 1:2], z_bank[i][:], ALU.mult, ALU.mult)
                 product(i, z_bank[i], w2q, xq)
                 nc.gpsimd.tensor_tensor(out=gated_base[i][:], in0=gated[i][:], in1=base_t[g][:, i % 2, :], op=ALU.add)
                 fused(q[i][:], zs[i][:], slope[i][:], tz1_bank[i][:], ALU.mult, ALU.add, q_sum[i][:])

from contextlib import ExitStack

import concourse.mybir as mybir

G, D, M, N = 2, 256, 256, 512
FLOPS = 4 * 2 * G * D * M * N

F32 = mybir.dt.float32
BF16 = mybir.dt.bfloat16
I32 = mybir.dt.int32
U32 = mybir.dt.uint32
U8 = mybir.dt.uint8
FP8X4 = mybir.dt.float8_e4m3fn_x4
ALU = mybir.AluOpType
ACT = mybir.ActivationFunctionType

P = 128
ROWS = 64
QUAD = 32
PACK = 4
TILES = G * M // P
HALF = N // 2
EPS = 0.05
X_SPLIT = 352
Y_SPLIT = 176


def tile_rows_pl_tnrowcentre_kernel(tc, x, w1, w2, gn, dx, og, base, out_0, out_1, out_2):
    nc = tc.nc
    with ExitStack() as ctx:
        sb = ctx.enter_context(tc.tile_pool(name="sb", bufs=1))
        ps = ctx.enter_context(tc.psum_pool(name="ps", bufs=1))
        ctx.enter_context(tc.manual_schedule())

        def new(name, shape, dtype=F32):
            return sb.tile(shape, dtype, name=name, align_bytes=64)

        def per_tile(name, width, dtype=F32):
            return [new("%s%d" % (name, i), [P, width], dtype) for i in range(TILES)]

        def per_group(name, shape, dtype=F32):
            return [new("%s%d" % (name, g), shape, dtype) for g in range(G)]

        def tiles_of(g):
            return (2 * g, 2 * g + 1)

        def column(group_tiles, i):
            return group_tiles[i // 2][:, i % 2:i % 2 + 1]

        def load_operand(name, src):
            raw = new(name, [P, PACK, src.shape[2]])
            nc.sync.dma_start(out=raw[:], in_=src.rearrange("g (p j) c -> (g p) j c", j=PACK))
            return raw

        x_raw = load_operand("x_raw", x)
        w1_raw = load_operand("w1_raw", w1)
        gain_rows = new("gain_rows", [P, TILES * QUAD])
        nc.vector.memset(gain_rows[:], 0.0)
        for r, src in enumerate((gn, og)):
            nc.sync.dma_start(out=gain_rows[r:P:QUAD, :].rearrange("q (i c) -> q i c", c=QUAD),
                              in_=src.rearrange("g (h q c) o -> q (g h) (c o)", h=2, c=QUAD))
        dx_raw = load_operand("dx_raw", dx)
        w2_raw = load_operand("w2_raw", w2)
        base_t = per_group("base", [P, 2, N])
        for g in range(G):
            nc.sync.dma_start(out=base_t[g][:], in_=base[g].rearrange("(h q) n -> q h n", h=2))

        def on_vector(out, in_):
            nc.vector.tensor_copy(out=out, in_=in_)

        def on_scalar(out, in_):
            nc.scalar.activation(out=out, in_=in_, func=ACT.Copy)

        def interleave(copy, dst, src, c0, c1):
            copy(dst[:, c0:c1, :].rearrange("p (c i) j -> p c j i", i=4),
                 src[:, :, c0:c1].rearrange("p j (c i) -> p c j i", i=4))

        def quantise(name, grouped, c0, c1):
            codes = new(name + "_codes", [P, c1 - c0], U32)
            scales = new(name + "_scales", [P, c1 - c0], U8)
            nc.vector.quantize_mx(out=codes[:].bitcast(FP8X4), scales=scales[:],
                                  in_=grouped[:, c0:c1, :].rearrange("p c j -> p (c j)"))
            return codes, scales

        banks = [[ps.tile([P, N], F32, name="bank%d%d" % (g, k)) for k in range(4)] for g in range(G)]
        z_bank = [banks[i // 2][i % 2] for i in range(TILES)]
        tz1_bank = [banks[i // 2][2 + i % 2] for i in range(TILES)]

        def product(i, bank, weights, moving):
            rows = slice(ROWS * (i // 2), ROWS * (i // 2 + 1))
            codes, scales = weights[i % 2]
            nc.tensor.matmul_mx(out=bank[:], lhsT=codes[rows, :].bitcast(FP8X4), lhsT_scale=scales[rows, :],
                                rhs=moving[0][rows, :].bitcast(FP8X4), rhs_scale=moving[1][rows, :],
                                start=True, stop=True)

        x_b, dx_b = new("x_b", [P, N, PACK], BF16), new("dx_b", [P, N, PACK], BF16)
        w1_b, w2_b = new("w1_b", [P, M, PACK], BF16), new("w2_b", [P, M, PACK], BF16)

        interleave(on_vector, x_b, x_raw, 0, X_SPLIT)
        interleave(on_scalar, x_b, x_raw, X_SPLIT, N)
        xq = quantise("xq", x_b, 0, N)
        interleave(on_scalar, w1_b, w1_raw, 0, P)
        w1q = [quantise("w1q0", w1_b, 0, P)]
        product(0, z_bank[0], w1q, xq)
        interleave(on_vector, w1_b, w1_raw, P, M)
        w1q.append(quantise("w1q1", w1_b, P, M))
        for i in range(1, TILES):
            product(i, z_bank[i], w1q, xq)

        gains = new("gains", [P, TILES, QUAD])
        by_root = new("by_root", [P, TILES, 8])
        by_mean = new("by_mean", [P, TILES, 2])
        minus_half = new("minus_half", [P, 2])
        nc.gpsimd.memset(minus_half[:], -0.5)
        nc.vector.transpose(out=gains[:].rearrange("p i c -> p (i c)"), in_=gain_rows[:])
        nc.vector.memset(by_root[:, :, 2], -float(N))
        nc.vector.memset(by_mean[:, :, 1], -1.0 / N)
        nc.vector.tensor_copy(out=by_mean[:, :, 0], in_=gains[:, :, 0])
        nc.vector.tensor_scalar(out=by_root[:, :, 0], in0=gains[:, :, 0], scalar1=-float(N), scalar2=None,
                                op0=ALU.mult)
        nc.vector.scalar_tensor_tensor(out=by_root[:, :, 1], in0=gains[:, :, 0], scalar=-1.0, in1=gains[:, :, 1],
                                       op0=ALU.mult, op1=ALU.mult)

        interleave(on_vector, dx_b, dx_raw, 0, N)
        dxq = quantise("dxq", dx_b, 0, N)
        for i in tiles_of(0):
            product(i, tz1_bank[i], w1q, dxq)

        zs, th, th_sq, q, gated, sech_z2, change, gated_base, y = [
            per_tile(name, N) for name in ("zs", "th", "th_sq", "q", "gated", "sech_z2", "change", "gated_base", "y")]
        squares, cov_terms = per_tile("squares", N), per_tile("cov_terms", N)
        cov, slope, q_sum, minus_q_mean, slope_fac = [
            per_tile(name, 1) for name in ("cov", "slope", "q_sum", "minus_q_mean", "slope_fac")]
        minus_mu, square_sum, variance, root = [
            per_group(name, [P, 2]) for name in ("minus_mu", "square_sum", "variance", "root")]
        rooted = per_tile("rooted", 4)
        y_round = per_tile("y_round", N, BF16)
        y_rows = per_group("y_rows", [P, PACK, HALF], BF16)
        y_b = per_group("y_b", [P, HALF, PACK], BF16)
        y_codes = per_group("y_codes", [P, HALF], U32)
        y_scales = new("y_scales", [P, HALF], U8)

        def scaled(out, in_, scale):
            nc.scalar.activation(out=out, in_=in_, func=ACT.Copy, scale=scale)

        def fused(out, in0, scalar, in1, op0, op1, accum_out=None):
            nc.vector.scalar_tensor_tensor(out=out, in0=in0, scalar=scalar, in1=in1, op0=op0, op1=op1,
                                           accum_out=accum_out)

        def copy_z1(g):
            for i in tiles_of(g):
                nc.scalar.activation(out=zs[i][:], in_=z_bank[i][:], func=ACT.Copy, scale=-1.0 / N,
                                     accum_out=column(minus_mu, i))

        def spread(g):
            for i in tiles_of(g):
                nc.scalar.activation(out=squares[i][:], in_=zs[i][:], func=ACT.Square, scale=-float(N),
                                     bias=column(minus_mu, i), accum_out=column(square_sum, i))
            nc.scalar.activation(out=variance[g][:], in_=square_sum[g][:], func=ACT.Copy, scale=1.0 / N, bias=EPS)
            nc.gpsimd.tensor_tensor(out=root[g][:], in0=variance[g][:], in1=minus_half[:], op=ALU.pow)

        def mean_terms(g):
            for i in tiles_of(g):
                scaled(by_root[:, i, 3:5], by_mean[:, i, :], column(minus_mu, i))

        def covariance(g):
            for i in tiles_of(g):
                fused(cov_terms[i][:], zs[i][:], by_root[:, i, 4:5], tz1_bank[i][:], ALU.add, ALU.mult, cov[i][:])

        def tanh(i):
            nc.scalar.activation(out=th[i][:], in_=zs[i][:], func=ACT.Tanh, scale=rooted[i][:, 0:1],
                                 bias=rooted[i][:, 3:4])

        def tanh_and_slope(g):
            first, second = tiles_of(g)
            for i in tiles_of(g):
                scaled(rooted[i][:], by_root[:, i, 0:4], column(root, i))
            tanh(first)
            for i in tiles_of(g):
                scaled(slope_fac[i][:], rooted[i][:, 2:3], column(root, i))
            scaled(slope[first][:], cov[first][:], slope_fac[first][:])
            tanh(second)
            scaled(slope[second][:], cov[second][:], slope_fac[second][:])

        def square_tanh(g):
            for i in tiles_of(g):
                nc.scalar.activation(out=th_sq[i][:], in_=th[i][:], func=ACT.Square)

        def empty_banks(g, w2q):
            for i in tiles_of(g):
                fused(gated[i][:], th[i][:], gains[:, i, 1:2], z_bank[i][:], ALU.mult, ALU.mult)
                product(i, z_bank[i], w2q, xq)
                nc.gpsimd.tensor_tensor(out=gated_base[i][:], in0=gated[i][:], in1=base_t[g][:, i % 2, :], op=ALU.add)
                fused(q[i][:], zs[i][:], slope[i][:], tz1_bank[i][:], ALU.mult, ALU.add, q_sum[i][:])
            for i in tiles_of(g):
                fused(sech_z2[i][:], th_sq[i][:], -1.0, z_bank[i][:], ALU.add, ALU.mult)

        def q_means(g):
            for i in tiles_of(g):
                scaled(minus_q_mean[i][:], q_sum[i][:], -1.0 / N)

        def changes(g):
            for i in tiles_of(g):
                fused(change[i][:], q[i][:], minus_q_mean[i][:], sech_z2[i][:], ALU.add, ALU.mult)

        def result(i, out):
            fused(out[:], change[i][:], rooted[i][:, 1:2], gated_base[i][:], ALU.mult, ALU.add)

        def store_result(i):
            nc.sync.dma_start(out=out_0[P * i:P * (i + 1), :], in_=y[i][:])

        def regroup(i, queues):
            for b in range(2):
                first = ROWS * b + QUAD * (i % 2)
                queues[b].dma_start(out=y_rows[i // 2][first:first + QUAD], in_=y_round[i][:, HALF * b:HALF * (b + 1)])

        def quantise_result(g, queues):
            nc.vector.quantize_mx(out=y_codes[g][:].bitcast(FP8X4), scales=y_scales[PACK * g:P, :],
                                  in_=y_b[g][:].rearrange("p c j -> p (c j)"))
            words = out_1.rearrange("s p n u -> (s p) (n u)").bitcast(I32)
            for b in range(2):
                queues[b].dma_start(out=words[ROWS * g:ROWS * (g + 1), HALF * b:HALF * (b + 1)],
                                    in_=y_codes[g][ROWS * b:ROWS * (b + 1), :].bitcast(I32))

        def store_scales(queues):
            rows = out_2.bitcast(I32).rearrange("s (g lo r) (b c) -> (s lo) b g r c", g=G, r=PACK, b=2)
            for quad in range(P // QUAD):
                b, lo = divmod(quad, 2)
                queues[lo].dma_start(out=rows[lo, b],
                                     in_=y_scales[QUAD * quad:QUAD * quad + G * PACK, :].bitcast(I32))

        one_queue, both_queues = (nc.sync, nc.sync), (nc.sync, nc.scalar)
        copy_z1(0)
        spread(0)
        mean_terms(0)
        copy_z1(1)
        interleave(on_vector, w2_b, w2_raw, 0, M)
        w2_codes, w2_scales = quantise("w2q", w2_b, 0, M)
        w2q = [(w2_codes[:, P * h:P * (h + 1)], w2_scales[:, P * h:P * (h + 1)]) for h in range(2)]
        for i in tiles_of(0):
            product(i, z_bank[i], w2q, dxq)
        for i in tiles_of(1):
            product(i, tz1_bank[i], w1q, dxq)
        for i in tiles_of(1):
            product(i, z_bank[i], w2q, dxq)
        covariance(0)
        tanh_and_slope(0)
        mean_terms(1)
        square_tanh(0)
        empty_banks(0, w2q)
        spread(1)
        q_means(0)
        covariance(1)
        tanh_and_slope(1)

        changes(0)
        for i in tiles_of(0):
            result(i, y[i])
            store_result(i)
        for i in tiles_of(0):
            on_scalar(y_round[i][:], y[i][:])
            regroup(i, one_queue)

        square_tanh(1)
        empty_banks(1, w2q)
        q_means(1)
        changes(1)
        for i in tiles_of(1):
            result(i, y_round[i])
            regroup(i, both_queues)
        for i in tiles_of(1):
            result(i, y[i])
            store_result(i)
        interleave(on_scalar, y_b[0], y_rows[0], 0, HALF)
        quantise_result(0, one_queue)
        interleave(on_vector, y_b[1], y_rows[1], 0, Y_SPLIT)
        interleave(on_scalar, y_b[1], y_rows[1], Y_SPLIT, HALF)
        quantise_result(1, both_queues)
        store_scales(both_queues)
